import numpy as np
import ml_dtypes


def mxq(x, axis, fmt="e4m3"):
    dtype, down = {"e4m3": (ml_dtypes.float8_e4m3fn, 7), "e5m2": (ml_dtypes.float8_e5m2, 14)}[fmt]
    v = np.moveaxis(np.asarray(x, np.float32).astype(ml_dtypes.bfloat16).astype(np.float64), axis, -1)
    blocks = v.reshape(v.shape[:-1] + (-1, 32))
    amax = np.abs(blocks).max(-1, keepdims=True)
    byte = np.maximum(np.where(amax > 0, np.frexp(amax)[1] - 1 + 127, 0) - down, 1)
    scale = np.exp2(byte - 127.0)
    codes = (blocks / scale).astype(np.float32).astype(dtype).astype(np.float64)
    return np.moveaxis((codes * scale).reshape(v.shape), -1, axis)


WIDE = False


def mx_kscale(k):
    if not WIDE:
        return np.ones(k)
    levels = np.array([10, -10, 5, -5, 0])
    if k % 512:
        return np.exp2(np.random.permutation(np.resize(levels, k // 32))).repeat(32)
    a = np.empty((k // 512, 16))
    for p in range(k // 512):
        a[p, :8] = np.random.permutation(np.resize(levels, 8))
        for g in range(8):
            far = levels[np.abs(levels - a[p, g]) >= 10]
            a[p, g + 8] = far[np.random.randint(len(far))]
    return np.exp2(a.ravel()).repeat(32)


def f64(x):
    return np.asarray(x).astype(np.float64)


def striped(idx):
    return np.tile(idx.reshape(-1, 16).T, (8, 1)).astype(np.uint16)


def unstriped(offs):
    return offs[:16].T.reshape(-1).astype(np.int64)


def pack_weight(w):
    k, n = w.shape
    w = f64(np.asarray(w, np.float32).astype(ml_dtypes.bfloat16)).reshape(k // 32, 32, n)
    amax = np.abs(w).max(1)
    byte = np.clip(np.where(amax > 0, np.frexp(amax)[1] - 1 + 127 - 7, 1), 1, 254)
    scaled = (w * np.exp2(127.0 - byte)[:, None, :]).reshape(k, n).astype(np.float32)
    words = np.ascontiguousarray(scaled.reshape(k // 512, 128, 4, n).transpose(0, 1, 3, 2)).astype(ml_dtypes.float8_e4m3fn).view(np.uint8)
    return words, np.ascontiguousarray(byte.astype(np.uint8).reshape(k // 512, 16, n))


def unpack_weight(words, scales):
    g, p, n, _ = words.shape
    vals = np.ascontiguousarray(words).view(ml_dtypes.float8_e4m3fn).astype(np.float64) * np.repeat(np.exp2(scales.astype(np.float64) - 127.0), 8, axis=1)[..., None]
    return vals.transpose(0, 1, 3, 2).reshape(g * 512, n)


def gelu(v):
    return 0.5 * v * (1.0 + np.tanh(np.sqrt(2.0 / np.pi) * (v + 0.044715 * v**3)))


K, T, S, N = 1536, 2048, 512, 128


def setup_inputs():
    n = np.random.standard_normal
    s = mx_kscale(K)[:, None]
    words, scales = pack_weight(n((K, N)) / np.sqrt(K) / s)
    return {
        "xT": (n((K, T)) * s).astype(np.float32),
        "w_words": words,
        "w_scales": scales,
        "b": (0.3 * n((N, 1))).astype(np.float32),
        "offs": striped(np.random.permutation(T)[:S]),
    }


def reference(xT, w_words, w_scales, b, offs):
    w = unpack_weight(w_words, w_scales)
    idx = unstriped(offs)
    xq = mxq(f64(xT)[:, idx], 0, "e4m3")
    y = w.T @ xq
    y = gelu(y + f64(b))
    return y

@@ -1,0 +1,101 @@
+from contextlib import ExitStack
+
+import concourse.mybir as mybir
+
+K, T, S, N = 1536, 2048, 512, 128
+FLOPS = 2 * K * S * N
+
+F32 = mybir.dt.float32
+BF16 = mybir.dt.bfloat16
+I32 = mybir.dt.int32
+U32 = mybir.dt.uint32
+U16 = mybir.dt.uint16
+U8 = mybir.dt.uint8
+FP8X4 = mybir.dt.float8_e4m3fn_x4
+
+P = 128
+PACK = 4
+K_PASS = P * PACK
+PASSES = K // K_PASS
+HALF = S // 2
+
+
+def tile_picked_pick_lin_gelu_sub_e_kernel(tc, xT, w_words, w_scales, b, offs, out):
+    nc = tc.nc
+    gelu = mybir.ActivationFunctionType.Gelu_apprx_tanh
+
+    with ExitStack() as ctx:
+        keep = ctx.enter_context(tc.tile_pool(name="keep", bufs=1))
+        psum = ctx.enter_context(tc.psum_pool(name="psum", bufs=1))
+
+        offsets = keep.tile([P, S // 16], U16, name="offsets")
+        bias = keep.tile([P, 1], F32, name="bias")
+        w_codes = keep.tile([P, PASSES, N], U32, name="w_codes", align_bytes=64)
+        w_planes = keep.tile([P, PASSES, N], U8, name="w_planes", align_bytes=64)
+        warm = keep.tile([P, 1], F32, name="warm")
+        warm_out = keep.tile([P, 1], F32, name="warm_out")
+
+        rows = xT.rearrange("(a p r) t -> a r p t", a=PASSES, p=P, r=PACK)
+        raw = [[keep.tile([P, T], F32, name=f"raw_{a}_{r}") for r in range(PACK)] for a in range(PASSES)]
+
+        for a in range(PASSES):
+            for r in range(PACK):
+                nc.sync.dma_start(out=raw[a][r][:], in_=rows[a, r])
+                if a == 0 and r == 0:
+                    nc.sync.dma_start(offsets[:], offs)
+
+        nc.gpsimd.memset(w_planes[:], 0)
+        scales_i32 = w_scales.bitcast(I32).rearrange("a q m -> q a m")
+        for q in range(4):
+            nc.sync.dma_start(out=w_planes[32 * q : 32 * q + 4, :, :].bitcast(I32), in_=scales_i32[4 * q : 4 * q + 4])
+        nc.sync.dma_start(out=w_codes[:].bitcast(I32), in_=w_words.rearrange("a p m r -> p a (m r)").bitcast(I32))
+        nc.sync.dma_start(out=bias[:], in_=b)
+
+        nc.vector.memset(warm[:], 0.0)
+        nc.scalar.activation(warm_out[:], warm[:], gelu)
+
+        grouped = [keep.tile([P, S, PACK], BF16, name=f"grouped_{a}", align_bytes=64) for a in range(PASSES)]
+        codes = [keep.tile([P, S], U32, name=f"codes_{a}", align_bytes=64) for a in range(PASSES)]
+        planes = [keep.tile([P, S], U8, name=f"planes_{a}", align_bytes=64) for a in range(PASSES)]
+        sums = [psum.tile([N, HALF], F32, name=f"sums_{h}") for h in range(2)]
+
+        def pick(a, r, c0, c1):
+            nc.vector.tensor_copy(grouped[a][:, c0:c1, r], raw[a][r][:].indirect(offsets[:, c0 // 16 : c1 // 16]))
+
+        def quantise(a, c0, c1):
+            nc.vector.quantize_mx(
+                out=codes[a][:, c0:c1].bitcast(FP8X4),
+                scales=planes[a][:, c0:c1],
+                in_=grouped[a][:, c0:c1, :].rearrange("p c r -> p (c r)"),
+            )
+
+        def multiply(a, h):
+            cols = slice(h * HALF, (h + 1) * HALF)
+            nc.tensor.matmul_mx(
+                out=sums[h][:],
+                lhsT=w_codes[:, a, :].bitcast(FP8X4),
+                lhsT_scale=w_planes[:, a, :],
+                rhs=codes[a][:, cols].bitcast(FP8X4),
+                rhs_scale=planes[a][:, cols],
+                start=(a == 0),
+                stop=(a == PASSES - 1),
+            )
+
+        for a in range(PASSES - 1):
+            for r in range(PACK):
+                pick(a, r, 0, S)
+            quantise(a, 0, S)
+            for h in range(2):
+                multiply(a, h)
+
+        a = PASSES - 1
+        for r in range(PACK - 1):
+            pick(a, r, 0, S)
+        for h in range(2):
+            pick(a, PACK - 1, h * HALF, (h + 1) * HALF)
+        for h in range(2):
+            quantise(a, h * HALF, (h + 1) * HALF)
+            multiply(a, h)
+            result = keep.tile([N, HALF], F32, name=f"result_{h}")
+            nc.scalar.activation(result[:], sums[h][:], gelu, bias=bias[:])
+            nc.sync.dma_start(out=out[:, h * HALF : (h + 1) * HALF], in_=result[:])

@@ -35,21 +35,28 @@ def tile_picked_pick_lin_gelu_sub_e_kernel(tc, xT, w_words, w_scales, b, offs, o
         warm = keep.tile([P, 1], F32, name="warm")
         warm_out = keep.tile([P, 1], F32, name="warm_out")
 
-        rows = xT.rearrange("(a p r) t -> a r p t", a=PASSES, p=P, r=PACK)
-        raw = [[keep.tile([P, T], F32, name=f"raw_{a}_{r}") for r in range(PACK)] for a in range(PASSES)]
-
+        planes_of = []
+        first_load = True
         for a in range(PASSES):
-            for r in range(PACK):
-                nc.sync.dma_start(out=raw[a][r][:], in_=rows[a, r])
-                if a == 0 and r == 0:
+            views = []
+            width = 2 if a < PASSES - 1 else 1
+            for r in range(0, PACK, width):
+                raw = keep.tile([P, width, T], F32, name=f"raw_{a}_{r}")
+                src = xT[a * K_PASS : (a + 1) * K_PASS, :].rearrange("(p r) t -> p r t", r=PACK)
+                nc.sync.dma_start(out=raw[:], in_=src[:, r : r + width, :])
+                if first_load:
                     nc.sync.dma_start(offsets[:], offs)
+                    first_load = False
+                views.extend(raw[:, i, :] for i in range(width))
+            planes_of.append(views)
+        for a in range(PASSES):
+            nc.sync.dma_start(out=w_codes[:, a, :].bitcast(I32), in_=w_words[a].rearrange("p m r -> p (m r)").bitcast(I32))
 
         nc.gpsimd.memset(w_planes[:], 0)
+        nc.gpsimd.dma_start(out=bias[:], in_=b)
         scales_i32 = w_scales.bitcast(I32).rearrange("a q m -> q a m")
         for q in range(4):
-            nc.sync.dma_start(out=w_planes[32 * q : 32 * q + 4, :, :].bitcast(I32), in_=scales_i32[4 * q : 4 * q + 4])
-        nc.sync.dma_start(out=w_codes[:].bitcast(I32), in_=w_words.rearrange("a p m r -> p a (m r)").bitcast(I32))
-        nc.sync.dma_start(out=bias[:], in_=b)
+            nc.gpsimd.dma_start(out=w_planes[32 * q : 32 * q + 4, :, :].bitcast(I32), in_=scales_i32[4 * q : 4 * q + 4])
 
         nc.vector.memset(warm[:], 0.0)
         nc.scalar.activation(warm_out[:], warm[:], gelu)
@@ -60,7 +67,7 @@ def tile_picked_pick_lin_gelu_sub_e_kernel(tc, xT, w_words, w_scales, b, offs, o
         sums = [psum.tile([N, HALF], F32, name=f"sums_{h}") for h in range(2)]
 
         def pick(a, r, c0, c1):
-            nc.vector.tensor_copy(grouped[a][:, c0:c1, r], raw[a][r][:].indirect(offsets[:, c0 // 16 : c1 // 16]))
+            nc.vector.tensor_copy(grouped[a][:, c0:c1, r], planes_of[a][r].indirect(offsets[:, c0 // 16 : c1 // 16]))
 
         def quantise(a, c0, c1):
             nc.vector.quantize_mx(

@@ -18,6 +18,7 @@ PACK = 4
 K_PASS = P * PACK
 PASSES = K // K_PASS
 HALF = S // 2
+LOAD_WIDTHS = ((2, 2), (2, 1, 1), (1, 1, 1, 1))
 
 
 def tile_picked_pick_lin_gelu_sub_e_kernel(tc, xT, w_words, w_scales, b, offs, out):
@@ -39,24 +40,24 @@ def tile_picked_pick_lin_gelu_sub_e_kernel(tc, xT, w_words, w_scales, b, offs, o
         first_load = True
         for a in range(PASSES):
             views = []
-            width = 2 if a < PASSES - 1 else 1
-            for r in range(0, PACK, width):
+            r = 0
+            for width in LOAD_WIDTHS[a]:
                 raw = keep.tile([P, width, T], F32, name=f"raw_{a}_{r}")
                 src = xT[a * K_PASS : (a + 1) * K_PASS, :].rearrange("(p r) t -> p r t", r=PACK)
                 nc.sync.dma_start(out=raw[:], in_=src[:, r : r + width, :])
                 if first_load:
                     nc.sync.dma_start(offsets[:], offs)
+                    nc.sync.dma_start(out=bias[:], in_=b)
                     first_load = False
                 views.extend(raw[:, i, :] for i in range(width))
+                r += width
             planes_of.append(views)
-        for a in range(PASSES):
-            nc.sync.dma_start(out=w_codes[:, a, :].bitcast(I32), in_=w_words[a].rearrange("p m r -> p (m r)").bitcast(I32))
-
         nc.gpsimd.memset(w_planes[:], 0)
-        nc.gpsimd.dma_start(out=bias[:], in_=b)
         scales_i32 = w_scales.bitcast(I32).rearrange("a q m -> q a m")
         for q in range(4):
-            nc.gpsimd.dma_start(out=w_planes[32 * q : 32 * q + 4, :, :].bitcast(I32), in_=scales_i32[4 * q : 4 * q + 4])
+            nc.sync.dma_start(out=w_planes[32 * q : 32 * q + 4, :, :].bitcast(I32), in_=scales_i32[4 * q : 4 * q + 4])
+        for a in range(PASSES):
+            nc.sync.dma_start(out=w_codes[:, a, :].bitcast(I32), in_=w_words[a].rearrange("p m r -> p (m r)").bitcast(I32))
 
         nc.vector.memset(warm[:], 0.0)
         nc.scalar.activation(warm_out[:], warm[:], gelu)

from contextlib import ExitStack

import concourse.mybir as mybir

K, T, S, N = 1536, 2048, 512, 128
FLOPS = 2 * K * S * N

F32 = mybir.dt.float32
BF16 = mybir.dt.bfloat16
I32 = mybir.dt.int32
U32 = mybir.dt.uint32
U16 = mybir.dt.uint16
U8 = mybir.dt.uint8
FP8X4 = mybir.dt.float8_e4m3fn_x4

P = 128
PACK = 4
K_PASS = P * PACK
PASSES = K // K_PASS
HALF = S // 2
LOAD_WIDTHS = ((2, 2), (2, 1, 1), (1, 1, 1, 1))


def tile_picked_pick_lin_gelu_sub_e_kernel(tc, xT, w_words, w_scales, b, offs, out):
    nc = tc.nc
    gelu = mybir.ActivationFunctionType.Gelu_apprx_tanh

    with ExitStack() as ctx:
        keep = ctx.enter_context(tc.tile_pool(name="keep", bufs=1))
        psum = ctx.enter_context(tc.psum_pool(name="psum", bufs=1))

        offsets = keep.tile([P, S // 16], U16, name="offsets")
        bias = keep.tile([P, 1], F32, name="bias")
        w_codes = keep.tile([P, PASSES, N], U32, name="w_codes", align_bytes=64)
        w_planes = keep.tile([P, PASSES, N], U8, name="w_planes", align_bytes=64)
        warm = keep.tile([P, 1], F32, name="warm")
        warm_out = keep.tile([P, 1], F32, name="warm_out")

        planes_of = []
        first_load = True
        for a in range(PASSES):
            views = []
            r = 0
            for width in LOAD_WIDTHS[a]:
                raw = keep.tile([P, width, T], F32, name=f"raw_{a}_{r}")
                src = xT[a * K_PASS : (a + 1) * K_PASS, :].rearrange("(p r) t -> p r t", r=PACK)
                nc.sync.dma_start(out=raw[:], in_=src[:, r : r + width, :])
                if first_load:
                    nc.sync.dma_start(offsets[:], offs)
                    nc.sync.dma_start(out=bias[:], in_=b)
                    first_load = False
                views.extend(raw[:, i, :] for i in range(width))
                r += width
            planes_of.append(views)
        nc.gpsimd.memset(w_planes[:], 0)
        scales_i32 = w_scales.bitcast(I32).rearrange("a q m -> q a m")
        for q in range(4):
            nc.sync.dma_start(out=w_planes[32 * q : 32 * q + 4, :, :].bitcast(I32), in_=scales_i32[4 * q : 4 * q + 4])
        for a in range(PASSES):
            nc.sync.dma_start(out=w_codes[:, a, :].bitcast(I32), in_=w_words[a].rearrange("p m r -> p (m r)").bitcast(I32))

        nc.vector.memset(warm[:], 0.0)
        nc.scalar.activation(warm_out[:], warm[:], gelu)

        grouped = [keep.tile([P, S, PACK], BF16, name=f"grouped_{a}", align_bytes=64) for a in range(PASSES)]
        codes = [keep.tile([P, S], U32, name=f"codes_{a}", align_bytes=64) for a in range(PASSES)]
        planes = [keep.tile([P, S], U8, name=f"planes_{a}", align_bytes=64) for a in range(PASSES)]
        sums = [psum.tile([N, HALF], F32, name=f"sums_{h}") for h in range(2)]

        def pick(a, r, c0, c1):
            nc.vector.tensor_copy(grouped[a][:, c0:c1, r], planes_of[a][r].indirect(offsets[:, c0 // 16 : c1 // 16]))

        def quantise(a, c0, c1):
            nc.vector.quantize_mx(
                out=codes[a][:, c0:c1].bitcast(FP8X4),
                scales=planes[a][:, c0:c1],
                in_=grouped[a][:, c0:c1, :].rearrange("p c r -> p (c r)"),
            )

        def multiply(a, h):
            cols = slice(h * HALF, (h + 1) * HALF)
            nc.tensor.matmul_mx(
                out=sums[h][:],
                lhsT=w_codes[:, a, :].bitcast(FP8X4),
                lhsT_scale=w_planes[:, a, :],
                rhs=codes[a][:, cols].bitcast(FP8X4),
                rhs_scale=planes[a][:, cols],
                start=(a == 0),
                stop=(a == PASSES - 1),
            )

        for a in range(PASSES - 1):
            for r in range(PACK):
                pick(a, r, 0, S)
            quantise(a, 0, S)
            for h in range(2):
                multiply(a, h)

        a = PASSES - 1
        for r in range(PACK - 1):
            pick(a, r, 0, S)
        for h in range(2):
            pick(a, PACK - 1, h * HALF, (h + 1) * HALF)
        for h in range(2):
            quantise(a, h * HALF, (h + 1) * HALF)
            multiply(a, h)
            result = keep.tile([N, HALF], F32, name=f"result_{h}")
            nc.scalar.activation(result[:], sums[h][:], gelu, bias=bias[:])
            nc.sync.dma_start(out=out[:, h * HALF : (h + 1) * HALF], in_=result[:])
